import numpy as np
import ml_dtypes


def mxq(x, axis, fmt="e4m3"):
    dtype, down = {"e4m3": (ml_dtypes.float8_e4m3fn, 7), "e5m2": (ml_dtypes.float8_e5m2, 14)}[fmt]
    v = np.moveaxis(np.asarray(x, np.float32).astype(ml_dtypes.bfloat16).astype(np.float64), axis, -1)
    blocks = v.reshape(v.shape[:-1] + (-1, 32))
    amax = np.abs(blocks).max(-1, keepdims=True)
    byte = np.maximum(np.where(amax > 0, np.frexp(amax)[1] - 1 + 127, 0) - down, 1)
    scale = np.exp2(byte - 127.0)
    codes = (blocks / scale).astype(np.float32).astype(dtype).astype(np.float64)
    return np.moveaxis((codes * scale).reshape(v.shape), -1, axis)


WIDE = False


def mx_kscale(k):
    if not WIDE:
        return np.ones(k)
    levels = np.array([30, -30])
    if k % 512:
        return np.exp2(np.random.permutation(np.resize(levels, k // 32))).repeat(32)
    a = np.empty((k // 512, 16))
    for p in range(k // 512):
        a[p, :8] = np.random.permutation(np.resize(levels, 8))
        for g in range(8):
            far = levels[np.abs(levels - a[p, g]) >= 10]
            a[p, g + 8] = far[np.random.randint(len(far))]
    return np.exp2(a.ravel()).repeat(32)


def f64(x):
    return np.asarray(x).astype(np.float64)


def striped(idx):
    return np.tile(np.asarray(idx).reshape(-1, 16).T, (8, 1)).astype(np.uint16)


def unstriped(offs):
    return offs[:16].T.reshape(-1).astype(np.int64)


def striped8(idx):
    return np.asarray(idx).reshape(8, -1, 16).transpose(0, 2, 1).reshape(128, -1).astype(np.uint16)


def unstriped8(offs):
    return offs.reshape(8, 16, -1).transpose(0, 2, 1).reshape(8, -1).astype(np.int64)


def pick8(x, idx, run):
    r = np.arange(len(x))
    return x[r[:, None], idx[r % (8 * run) // run]]


E2M1 = np.array([0.0, 0.5, 1.0, 1.5, 2.0, 3.0, 4.0, 6.0, -0.0, -0.5, -1.0, -1.5, -2.0, -3.0, -4.0, -6.0])


def pack_weight(w, fmt):
    k, n = w.shape
    w = f64(np.asarray(w, np.float32).astype(ml_dtypes.bfloat16)).reshape(k // 32, 32, n)
    amax = np.abs(w).max(1)
    if fmt in ("e4m3", "e5m2"):
        byte = np.frexp(amax)[1] - 1 + 127 - (7 if fmt == "e4m3" else 14)
    else:
        mant, ex = np.frexp(amax / 6.0)
        byte = np.where(mant > 0.5, ex, ex - 1) + 127
    byte = np.clip(np.where(amax > 0, byte, 1), 1, 254)
    scaled = (w * np.exp2(127.0 - byte)[:, None, :]).reshape(k, n).astype(np.float32)
    by_word = np.ascontiguousarray(scaled.reshape(k // 512, 128, 4, n).transpose(0, 1, 3, 2))
    if fmt in ("e4m3", "e5m2"):
        words = by_word.astype(ml_dtypes.float8_e4m3fn if fmt == "e4m3" else ml_dtypes.float8_e5m2).view(np.uint8)
    else:
        c = by_word.astype(ml_dtypes.float4_e2m1fn).view(np.uint8) & 0xF
        words = (c[..., 0::2] | (c[..., 1::2] << 4)).reshape(k // 512, 128, 2 * n)
    return np.ascontiguousarray(words), np.ascontiguousarray(byte.astype(np.uint8).reshape(k // 512, 16, n))


def unpack_weight(words, scales, fmt):
    g, _, n = scales.shape
    words = np.ascontiguousarray(words).reshape(g, 128, n, -1)
    if fmt in ("e4m3", "e5m2"):
        vals = words.view(ml_dtypes.float8_e4m3fn if fmt == "e4m3" else ml_dtypes.float8_e5m2).astype(np.float64)
    else:
        nib = np.empty((g, 128, n, 4), np.uint8)
        nib[..., 0::2] = words & 0xF
        nib[..., 1::2] = words >> 4
        vals = E2M1[nib]
    vals = vals * np.repeat(np.exp2(scales.astype(np.float64) - 127.0), 8, axis=1)[..., None]
    return vals.transpose(0, 1, 3, 2).reshape(g * 512, n)


K, T, J, R, F, Z, C, O, D, N = 512, 1024, 256, 512, 512, 1024, 512, 256, 512, 256


def setup_inputs():
    n = np.random.standard_normal
    idx = np.random.permutation(T)[:J]
    idx2 = np.random.permutation(Z)[:J]
    idx3 = np.stack([np.random.permutation(C)[:J] for _ in range(8)])
    idx4 = np.stack([np.random.permutation(C)[:O] for _ in range(8)])
    fk = mx_kscale(K)
    ff = mx_kscale(F)
    fr = mx_kscale(R)
    xtp = pack_weight(n((K, T)) / fk[:, None], "e2m1")
    xop = pack_weight(n((F, Z)) / ff[:, None], "e5m2")
    wp = pack_weight(n((K, R)) * 1 / np.sqrt(K) * fk[:, None] * fr, "e5m2")
    w2p = pack_weight(n((K, R)) * 1 / np.sqrt(K) * fk[:, None] * fr, "e4m3")
    w0p = pack_weight(n((F, R)) * 1 / np.sqrt(F) * ff[:, None] * fr, "e4m3")
    wbp = pack_weight(n((R, N)) * 1 / np.sqrt(R) / fr[:, None], "e4m3")
    return {
        "xt_words": xtp[0],
        "xt_scales": xtp[1],
        "xo_words": xop[0],
        "xo_scales": xop[1],
        "w_words": wp[0],
        "w_scales": wp[1],
        "w2_words": w2p[0],
        "w2_scales": w2p[1],
        "w0_words": w0p[0],
        "w0_scales": w0p[1],
        "wb_words": wbp[0],
        "wb_scales": wbp[1],
        "offs": striped(idx),
        "offs2": striped(idx2),
        "offs3": striped8(idx3),
        "offs4": striped8(idx4),
    }


def reference(xt_words, xt_scales, xo_words, xo_scales, w_words, w_scales, w2_words, w2_scales, w0_words, w0_scales, wb_words, wb_scales, offs, offs2, offs3, offs4):
    idx = unstriped(offs)
    idx2 = unstriped(offs2)
    idx3 = unstriped8(offs3)
    idx4 = unstriped8(offs4)
    xtu = unpack_weight(xt_words, xt_scales, "e2m1")
    xou = unpack_weight(xo_words, xo_scales, "e5m2")
    wu = unpack_weight(w_words, w_scales, "e5m2")
    w2u = unpack_weight(w2_words, w2_scales, "e4m3")
    w0u = unpack_weight(w0_words, w0_scales, "e4m3")
    wbu = unpack_weight(wb_words, wb_scales, "e4m3")
    xtidxg = xtu[:, idx]
    a = wu.T @ xtidxg
    xoidx2g = xou[:, idx2]
    b = w2u.T @ xtidxg + w0u.T @ xoidx2g
    pa = np.zeros((R, C))
    pa[np.arange(R)[:, None], idx3[np.arange(R) % 512 // 64]] = a
    h1 = pick8(pa, idx4, 64)
    hid = np.concatenate([b, h1], axis=1)
    hidq = mxq(hid, 0, "e5m2")
    p = wbu.T @ hidq
    return p

@@ -1,0 +1,235 @@
+from contextlib import ExitStack
+
+import concourse.mybir as mybir
+from concourse.masks import make_identity
+
+F32 = mybir.dt.float32
+BF16 = mybir.dt.bfloat16
+I32 = mybir.dt.int32
+U32 = mybir.dt.uint32
+U16 = mybir.dt.uint16
+U8 = mybir.dt.uint8
+E4M3 = mybir.dt.float8_e4m3fn_x4
+E5M2 = mybir.dt.float8_e5m2_x4
+E2M1 = mybir.dt.float4_e2m1fn_x4
+COPY = mybir.ActivationFunctionType.Copy
+
+P = 128
+T, J, R, C, O, N = 1024, 256, 512, 512, 256, 256
+FLOPS = 536870912
+
+
+def words_of(dram):
+    return dram[0].rearrange("p c r -> p (c r)").bitcast(I32)
+
+
+def load_plane(queue, plane, dram):
+    rows = dram[0].bitcast(I32)
+    for q in range(4):
+        queue.dma_start(out=plane[32 * q : 32 * q + 4, :].bitcast(I32), in_=rows[4 * q : 4 * q + 4, :])
+
+
+def load_folded(queue, folded, dram, first=0):
+    rows = dram[0].bitcast(I32).rearrange("(h b r) n -> b r h n", h=2, b=2)
+    width = rows.shape[3]
+    for b in range(2):
+        halves = folded[32 * b : 32 * b + 4, :].bitcast(I32).rearrange("p (h n) -> p h n", h=2)
+        queue.dma_start(out=halves[:, :, first : first + width], in_=rows[b])
+
+
+def unfold(nc, folded):
+    words = folded[:].bitcast(I32)
+    half = words.shape[1] // 2
+    nc.vector.tensor_copy(out=words[64:128, 0:half], in_=words[0:64, half : 2 * half])
+
+
+def unfold_into(nc, plane, folded):
+    words = folded[:].bitcast(I32)
+    half = words.shape[1] // 2
+    for h in range(2):
+        nc.vector.tensor_copy(out=plane[64 * h : 64 * h + 64, :].bitcast(I32), in_=words[0:64, half * h : half * (h + 1)])
+
+
+def tile_list_joinedreads_kernel(
+    tc, xt_words, xt_scales, xo_words, xo_scales, w_words, w_scales, w2_words, w2_scales,
+    w0_words, w0_scales, wb_words, wb_scales, offs, offs2, offs3, offs4, out,
+):
+    nc = tc.nc
+    with ExitStack() as ctx:
+        lists = ctx.enter_context(tc.tile_pool(name="lists", bufs=1))
+        sb = ctx.enter_context(tc.tile_pool(name="sb", bufs=1))
+        ps = ctx.enter_context(tc.psum_pool(name="ps", bufs=1))
+
+        def tile(name, width, dtype, tag=None):
+            return sb.tile([P, width], dtype, name=name, tag=tag or name, align_bytes=64)
+
+        def bank(name, tag=None):
+            return ps.tile([P, 512], F32, name=name, tag=tag or name)
+
+        l1 = lists.tile([P, 16], U16, name="l1")
+        l2 = lists.tile([P, 16], U16, name="l2")
+        l3 = lists.tile([P, 16], U16, name="l3")
+        l4 = lists.tile([P, 16], U16, name="l4")
+
+        xt_w = tile("xt_w", T, U16)
+        xt_s = tile("xt_s", T, U8)
+        xo_w = tile("xo_w", T, U32)
+        xo_s = tile("xo_s", T, U8)
+        w_w = tile("w_w", R, U32)
+        w_s = tile("w_s", 2 * R, U8)
+        w2_w = tile("w2_w", R, U32)
+        w0_w = tile("w0_w", R, U32)
+        b_f = tile("b_f", 4 * R, U8, tag="fold_then_h01")
+        xt_f = tile("xt_f", 2 * T, U8)
+        wb_w = tile("wb_w", N, U32)
+        wb_s = tile("wb_s", N, U8)
+        board = [tile("board%d" % t, C, F32) for t in range(4)]
+        ident = tile("ident", P, F32)
+
+        nc.gpsimd.memset(xt_f[:].bitcast(I32), 0)
+        for plane in (w_s, xo_s, b_f):
+            nc.vector.memset(plane[:].bitcast(I32), 0)
+
+        nc.sync.dma_start(l1[:], offs)
+        nc.sync.dma_start(l3[:], offs3)
+        load_folded(nc.sync, xt_f, xt_scales)
+        load_folded(nc.sync, w_s, w_scales)
+        nc.sync.dma_start(out=xt_w[:].bitcast(I32), in_=xt_words[0].bitcast(I32))
+        nc.sync.dma_start(out=w_w[:].bitcast(I32), in_=words_of(w_words))
+        load_plane(nc.sync, xo_s, xo_scales)
+        nc.sync.dma_start(l2[:], offs2)
+        nc.sync.dma_start(out=xo_w[:].bitcast(I32), in_=words_of(xo_words))
+        nc.sync.dma_start(out=w2_w[:].bitcast(I32), in_=words_of(w2_words))
+        nc.sync.dma_start(out=w0_w[:].bitcast(I32), in_=words_of(w0_words))
+        load_folded(nc.sync, b_f, w2_scales)
+        load_folded(nc.sync, b_f, w0_scales, first=R // 4)
+        nc.sync.dma_start(l4[:], offs4)
+        nc.sync.dma_start(out=wb_w[:].bitcast(I32), in_=words_of(wb_words))
+        load_plane(nc.sync, wb_s, wb_scales)
+
+        for t in range(3):
+            nc.vector.memset(board[t][:], 0.0)
+        make_identity(nc, ident[:])
+        nc.gpsimd.memset(board[3][:], 0.0)
+
+        xt_gw = tile("xt_gw", J, U16)
+        xt_gs = tile("xt_gs", J, U8)
+        unfold_into(nc, xt_s, xt_f)
+        unfold(nc, w_s)
+        nc.vector.tensor_copy(out=xt_gs[:], in_=xt_s[:].indirect(l1[:]))
+        nc.vector.tensor_copy(out=xt_gw[:], in_=xt_w[:].indirect(l1[:]))
+
+        w_pw = [tile("w_pw%d" % t, P, U32) for t in range(4)]
+        w_ps = [tile("w_ps%d" % t, P, U8) for t in range(4)]
+        w_w4 = w_w[:].rearrange("p (m t) -> p t m", t=4)
+        w_s4 = w_s[:, 0:R].rearrange("p (m t) -> p t m", t=4)
+        for t in range(4):
+            nc.gpsimd.tensor_copy(out=w_ps[t][:], in_=w_s4[:, t, :])
+            nc.gpsimd.tensor_copy(out=w_pw[t][:], in_=w_w4[:, t, :])
+
+        a_sb = tile("a_sb", 4 * J, F32)
+        for t in range(4):
+            a_ps = bank("a%d" % t, tag="a_even" if t % 2 == 0 else "a_odd")
+            nc.tensor.matmul_mx(
+                out=a_ps[:, 0:J],
+                lhsT=w_pw[t][:].bitcast(E5M2),
+                lhsT_scale=w_ps[t][:],
+                rhs=xt_gw[:].bitcast(E2M1),
+                rhs_scale=xt_gs[:],
+                start=True,
+                stop=True,
+            )
+            nc.vector.tensor_copy(out=a_sb[:, J * t : J * (t + 1)], in_=a_ps[:, 0:J])
+        for t in range(4):
+            nc.scalar.activation(out=board[t][:].indirect(l3[:]), in_=a_sb[:, J * t : J * (t + 1)], func=COPY)
+
+        xo_gw = tile("xo_gw", J, U32, tag="w_pw0")
+        xo_gs = tile("xo_gs", J, U8, tag="w_ps0")
+        nc.vector.tensor_copy(out=xo_gs[:], in_=xo_s[:].indirect(l2[:]))
+        nc.vector.tensor_copy(out=xo_gw[:], in_=xo_w[:].indirect(l2[:]))
+        b_s = tile("b_s", 2 * R, U8, tag="w_pw1")
+        w2_s, w0_s = b_s[:, 0:R], b_s[:, R : 2 * R]
+        unfold_into(nc, b_s, b_f)
+
+        h01 = tile("h01", 2 * O, F32, tag="fold_then_h01")
+        h23 = tile("h23", 128 + 2 * O, F32)
+        nc.vector.tensor_copy(out=h01[:, 0:O], in_=board[0][:].indirect(l4[:]))
+
+        bt_sb0 = tile("bt_sb0", R // 2, F32)
+        bt_words = [h01[:, O : 2 * O], bt_sb0[:]]
+        turned = bank("turned")
+        for h in range(2):
+            cols = slice(P * h, P * (h + 1))
+            bt = bank("bt%d" % h)
+            nc.tensor.matmul_mx(
+                out=bt[:], lhsT=xt_gw[:, cols].bitcast(E2M1), lhsT_scale=xt_gs[:, cols],
+                rhs=w2_w[:].bitcast(E4M3), rhs_scale=w2_s, start=True, stop=False,
+            )
+            nc.tensor.matmul_mx(
+                out=bt[:], lhsT=xo_gw[:, cols].bitcast(E5M2), lhsT_scale=xo_gs[:, cols],
+                rhs=w0_w[:].bitcast(E4M3), rhs_scale=w0_s, start=False, stop=True,
+            )
+            nc.vector.tensor_copy(
+                out=bt_words[h].bitcast(BF16).rearrange("j (u p e) -> j u p e", u=2, e=2),
+                in_=bt[:].rearrange("j (p u e) -> j u p e", u=2, e=2),
+            )
+        for h in range(2):
+            for u in range(2):
+                k = 2 * h + u
+                nc.tensor.transpose(turned[:, P * k : P * (k + 1)], bt_words[h][:, P * u : P * (u + 1)], ident[:])
+        hid_b = h23[:, 0:512]
+        nc.vector.tensor_copy(
+            out=hid_b.rearrange("p (h j u) -> p h j u", h=2, u=2),
+            in_=turned[:].rearrange("p (h u j) -> p h j u", h=2, u=2),
+        )
+        nc.vector.tensor_copy(out=h01[:, O : 2 * O], in_=board[1][:].indirect(l4[:]))
+        qb_w = tile("qb_w", J, U32)
+        qb_s = tile("qb_s", J, U8)
+        nc.vector.quantize_mx(out=qb_w[:].bitcast(E5M2), scales=qb_s[:], in_=hid_b.bitcast(BF16))
+        out_b = bank("out_b")
+        for m in range(2):
+            nc.tensor.matmul_mx(
+                out=out_b[:, J * m : J * (m + 1)],
+                lhsT=wb_w[:, P * m : P * (m + 1)].bitcast(E4M3), lhsT_scale=wb_s[:, P * m : P * (m + 1)],
+                rhs=qb_w[:].bitcast(E5M2), rhs_scale=qb_s[:], start=True, stop=True,
+            )
+
+        hid_h = tile("hid_h", 4 * O, BF16)
+        hid_h4 = hid_h[:].rearrange("p (o t) -> p o t", t=4)
+        nc.vector.tensor_copy(out=hid_h4[:, :, 0:2], in_=h01[:].rearrange("p (t o) -> p o t", t=2))
+        h2 = h23[:, 128 : 128 + O]
+        h3 = h23[:, 128 + O : 128 + 2 * O]
+        nc.vector.tensor_copy(out=h2, in_=board[2][:].indirect(l4[:]))
+        nc.vector.tensor_copy(out=h3[:, 0:128], in_=board[3][:].indirect(l4[:, 0:8]))
+        nc.scalar.activation(out=h3[:, 128:256], in_=board[3][:].indirect(l4[:, 8:16]), func=COPY)
+
+        out_v = out.rearrange("(m p) d -> p m d", m=2)
+        res_b = tile("res_b", 2 * J, F32)
+        nc.scalar.copy(out=res_b[:], in_=out_b[:])
+        nc.sync.dma_start(out=out_v[:, :, 0:J], in_=res_b[:].rearrange("p (m d) -> p m d", m=2))
+
+        pairs23 = h23[:, 128 : 128 + 2 * O].rearrange("p (t o) -> p o t", t=2)
+        qh_w = tile("qh_w", O, U32)
+        qh_s = tile("qh_s", O, U8)
+        for h in range(2):
+            cols = slice(P * h, P * (h + 1))
+            nc.vector.tensor_copy(out=hid_h4[:, cols, 2:4], in_=pairs23[:, cols, :])
+        for h in range(2):
+            cols = slice(P * h, P * (h + 1))
+            nc.vector.quantize_mx(
+                out=qh_w[:, cols].bitcast(E5M2), scales=qh_s[:, cols], in_=hid_h[:, 512 * h : 512 * (h + 1)]
+            )
+        out_h = [bank("out_h0"), bank("out_h1")]
+        res_h = [tile("res_h%d" % h, 2 * P, F32) for h in range(2)]
+        for h in range(2):
+            cols = slice(P * h, P * (h + 1))
+            for m in range(2):
+                nc.tensor.matmul_mx(
+                    out=out_h[h][:, P * m : P * (m + 1)],
+                    lhsT=wb_w[:, P * m : P * (m + 1)].bitcast(E4M3), lhsT_scale=wb_s[:, P * m : P * (m + 1)],
+                    rhs=qh_w[:, cols].bitcast(E5M2), rhs_scale=qh_s[:, cols], start=True, stop=True,
+                )
+        nc.scalar.copy(out=res_h[0][:], in_=out_h[0][:, 0 : 2 * P])
+        nc.scalar.dma_start(out=out_v[:, :, J : J + P], in_=res_h[0][:].rearrange("p (m d) -> p m d", m=2))
+        nc.vector.tensor_copy(out=res_h[1][:], in_=out_h[1][:, 0 : 2 * P])
+        nc.sync.dma_start(out=out_v[:, :, J + P : J + 2 * P], in_=res_h[1][:].rearrange("p (m d) -> p m d", m=2))

@@ -23,31 +23,13 @@ def words_of(dram):
     return dram[0].rearrange("p c r -> p (c r)").bitcast(I32)
 
 
-def load_plane(queue, plane, dram):
-    rows = dram[0].bitcast(I32)
-    for q in range(4):
-        queue.dma_start(out=plane[32 * q : 32 * q + 4, :].bitcast(I32), in_=rows[4 * q : 4 * q + 4, :])
+def load_rows(queue, staged, dram):
+    queue.dma_start(out=staged, in_=dram[0].bitcast(I32).rearrange("(q r) n -> r q n", q=4))
 
 
-def load_folded(queue, folded, dram, first=0):
-    rows = dram[0].bitcast(I32).rearrange("(h b r) n -> b r h n", h=2, b=2)
-    width = rows.shape[3]
-    for b in range(2):
-        halves = folded[32 * b : 32 * b + 4, :].bitcast(I32).rearrange("p (h n) -> p h n", h=2)
-        queue.dma_start(out=halves[:, :, first : first + width], in_=rows[b])
-
-
-def unfold(nc, folded):
-    words = folded[:].bitcast(I32)
-    half = words.shape[1] // 2
-    nc.vector.tensor_copy(out=words[64:128, 0:half], in_=words[0:64, half : 2 * half])
-
-
-def unfold_into(nc, plane, folded):
-    words = folded[:].bitcast(I32)
-    half = words.shape[1] // 2
-    for h in range(2):
-        nc.vector.tensor_copy(out=plane[64 * h : 64 * h + 64, :].bitcast(I32), in_=words[0:64, half * h : half * (h + 1)])
+def spread_rows(nc, plane, staged, first):
+    for q in range(first, 4):
+        nc.vector.tensor_copy(out=plane[32 * q : 32 * q + 4, :], in_=staged[:, q, :])
 
 
 def tile_list_joinedreads_kernel(
@@ -73,51 +55,57 @@ def tile_list_joinedreads_kernel(
 
         xt_w = tile("xt_w", T, U16)
         xt_s = tile("xt_s", T, U8)
-        xo_w = tile("xo_w", T, U32)
+        xo_w = tile("xo_w", T, U32, tag="fold_then_h01")
         xo_s = tile("xo_s", T, U8)
         w_w = tile("w_w", R, U32)
-        w_s = tile("w_s", 2 * R, U8)
+        w_s = tile("w_s", R, U8)
         w2_w = tile("w2_w", R, U32)
         w0_w = tile("w0_w", R, U32)
-        b_f = tile("b_f", 4 * R, U8, tag="fold_then_h01")
-        xt_f = tile("xt_f", 2 * T, U8)
         wb_w = tile("wb_w", N, U32)
-        wb_s = tile("wb_s", N, U8)
+
+        def staging(name, width):
+            rows = sb.tile([4, width], I32, name=name)
+            return rows[:].rearrange("p (q n) -> p q n", q=4)
+
+        xt_rows, xo_rows, w_rows = staging("xt_rows", T), staging("xo_rows", T), staging("w_rows", R)
+        late = tile("late", 4 * (2 * R + N), U8)
+        late_rows = late[0:4, :].bitcast(I32).rearrange("p (q n) -> p q n", q=4)
+        w2_s, w0_s, wb_s = late[:, 0:R], late[:, R : 2 * R], late[:, 2 * R : 2 * R + N]
         board = [tile("board%d" % t, C, F32) for t in range(4)]
         ident = tile("ident", P, F32)
 
-        nc.gpsimd.memset(xt_f[:].bitcast(I32), 0)
-        for plane in (w_s, xo_s, b_f):
-            nc.vector.memset(plane[:].bitcast(I32), 0)
-
         nc.sync.dma_start(l1[:], offs)
-        nc.sync.dma_start(l3[:], offs3)
-        load_folded(nc.sync, xt_f, xt_scales)
-        load_folded(nc.sync, w_s, w_scales)
+        load_rows(nc.sync, xt_rows, xt_scales)
+        load_rows(nc.sync, w_rows, w_scales)
+        nc.sync.dma_start(l2[:], offs2)
         nc.sync.dma_start(out=xt_w[:].bitcast(I32), in_=xt_words[0].bitcast(I32))
         nc.sync.dma_start(out=w_w[:].bitcast(I32), in_=words_of(w_words))
-        load_plane(nc.sync, xo_s, xo_scales)
-        nc.sync.dma_start(l2[:], offs2)
+        load_rows(nc.sync, xo_rows, xo_scales)
         nc.sync.dma_start(out=xo_w[:].bitcast(I32), in_=words_of(xo_words))
+        nc.sync.dma_start(l3[:], offs3)
         nc.sync.dma_start(out=w2_w[:].bitcast(I32), in_=words_of(w2_words))
         nc.sync.dma_start(out=w0_w[:].bitcast(I32), in_=words_of(w0_words))
-        load_folded(nc.sync, b_f, w2_scales)
-        load_folded(nc.sync, b_f, w0_scales, first=R // 4)
+        load_rows(nc.sync, late_rows[:, :, 0:128], w2_scales)
+        load_rows(nc.sync, late_rows[:, :, 128:256], w0_scales)
+        load_rows(nc.sync, late_rows[:, :, 256:320], wb_scales)
         nc.sync.dma_start(l4[:], offs4)
         nc.sync.dma_start(out=wb_w[:].bitcast(I32), in_=words_of(wb_words))
-        load_plane(nc.sync, wb_s, wb_scales)
 
-        for t in range(3):
-            nc.vector.memset(board[t][:], 0.0)
+        for plane in (xt_s, w_s, xo_s):
+            nc.vector.memset(plane[:].bitcast(I32), 0)
+        nc.vector.memset(board[0][:], 0.0)
+        for t in range(1, 4):
+            nc.gpsimd.memset(board[t][:], 0.0)
         make_identity(nc, ident[:])
-        nc.gpsimd.memset(board[3][:], 0.0)
 
         xt_gw = tile("xt_gw", J, U16)
         xt_gs = tile("xt_gs", J, U8)
-        unfold_into(nc, xt_s, xt_f)
-        unfold(nc, w_s)
-        nc.vector.tensor_copy(out=xt_gs[:], in_=xt_s[:].indirect(l1[:]))
-        nc.vector.tensor_copy(out=xt_gw[:], in_=xt_w[:].indirect(l1[:]))
+        spread_rows(nc, xt_s[:].bitcast(I32), xt_rows, 0)
+        spread_rows(nc, w_s[:].bitcast(I32), w_rows, 0)
+        for h in range(2):
+            entries = l1[:, 8 * h : 8 * (h + 1)]
+            nc.vector.tensor_copy(out=xt_gs[:, P * h : P * (h + 1)], in_=xt_s[:].indirect(entries))
+            nc.vector.tensor_copy(out=xt_gw[:, P * h : P * (h + 1)], in_=xt_w[:].indirect(entries))
 
         w_pw = [tile("w_pw%d" % t, P, U32) for t in range(4)]
         w_ps = [tile("w_ps%d" % t, P, U8) for t in range(4)]
@@ -125,38 +113,46 @@ def tile_list_joinedreads_kernel(
         w_s4 = w_s[:, 0:R].rearrange("p (m t) -> p t m", t=4)
         for t in range(4):
             nc.gpsimd.tensor_copy(out=w_ps[t][:], in_=w_s4[:, t, :])
-            nc.gpsimd.tensor_copy(out=w_pw[t][:], in_=w_w4[:, t, :])
+            nc.scalar.copy(out=w_pw[t][:], in_=w_w4[:, t, :])
 
         a_sb = tile("a_sb", 4 * J, F32)
-        for t in range(4):
-            a_ps = bank("a%d" % t, tag="a_even" if t % 2 == 0 else "a_odd")
-            nc.tensor.matmul_mx(
-                out=a_ps[:, 0:J],
-                lhsT=w_pw[t][:].bitcast(E5M2),
-                lhsT_scale=w_ps[t][:],
-                rhs=xt_gw[:].bitcast(E2M1),
-                rhs_scale=xt_gs[:],
-                start=True,
-                stop=True,
-            )
-            nc.vector.tensor_copy(out=a_sb[:, J * t : J * (t + 1)], in_=a_ps[:, 0:J])
-        for t in range(4):
-            nc.scalar.activation(out=board[t][:].indirect(l3[:]), in_=a_sb[:, J * t : J * (t + 1)], func=COPY)
+        pieces = [(0, 0, P), (0, P, J), (1, 0, J), (2, 0, J), (3, 0, J)]
+        groups = [pieces[0:1], pieces[1:3], pieces[3:5]]
+        for g, group in enumerate(groups):
+            a_ps = bank("a%d" % g)
+            first = J * group[0][0] + group[0][1]
+            for t, lo, hi in group:
+                nc.tensor.matmul_mx(
+                    out=a_ps[:, J * t + lo - first : J * t + hi - first],
+                    lhsT=w_pw[t][:].bitcast(E5M2),
+                    lhsT_scale=w_ps[t][:],
+                    rhs=xt_gw[:, lo:hi].bitcast(E2M1),
+                    rhs_scale=xt_gs[:, lo:hi],
+                    start=True,
+                    stop=True,
+                )
+            width = sum(hi - lo for t, lo, hi in group)
+            nc.scalar.copy(out=a_sb[:, first : first + width], in_=a_ps[:, 0:width])
+            for t, lo, hi in group:
+                nc.scalar.activation(
+                    out=board[t][:].indirect(l3[:, lo // 16 : hi // 16]),
+                    in_=a_sb[:, J * t + lo : J * t + hi],
+                    func=COPY,
+                )
 
-        xo_gw = tile("xo_gw", J, U32, tag="w_pw0")
-        xo_gs = tile("xo_gs", J, U8, tag="w_ps0")
+        xo_gw = tile("xo_gw", J, U32)
+        xo_gs = tile("xo_gs", J, U8)
+        spread_rows(nc, xo_s[:].bitcast(I32), xo_rows, 0)
         nc.vector.tensor_copy(out=xo_gs[:], in_=xo_s[:].indirect(l2[:]))
         nc.vector.tensor_copy(out=xo_gw[:], in_=xo_w[:].indirect(l2[:]))
-        b_s = tile("b_s", 2 * R, U8, tag="w_pw1")
-        w2_s, w0_s = b_s[:, 0:R], b_s[:, R : 2 * R]
-        unfold_into(nc, b_s, b_f)
+        spread_rows(nc, late[:, 0 : 2 * R + N].bitcast(I32), late_rows, 1)
 
-        h01 = tile("h01", 2 * O, F32, tag="fold_then_h01")
-        h23 = tile("h23", 128 + 2 * O, F32)
-        nc.vector.tensor_copy(out=h01[:, 0:O], in_=board[0][:].indirect(l4[:]))
+        pitch = 640
+        reads = tile("reads", 4 * pitch, F32, tag="fold_then_h01")
+        h1 = [reads[:, pitch * t : pitch * t + O] for t in range(4)]
+        nc.vector.tensor_copy(out=h1[0], in_=board[0][:].indirect(l4[:]))
 
-        bt_sb0 = tile("bt_sb0", R // 2, F32)
-        bt_words = [h01[:, O : 2 * O], bt_sb0[:]]
+        bt_words = [h1[1], h1[2]]
         turned = bank("turned")
         for h in range(2):
             cols = slice(P * h, P * (h + 1))
@@ -177,12 +173,12 @@ def tile_list_joinedreads_kernel(
             for u in range(2):
                 k = 2 * h + u
                 nc.tensor.transpose(turned[:, P * k : P * (k + 1)], bt_words[h][:, P * u : P * (u + 1)], ident[:])
-        hid_b = h23[:, 0:512]
+        hid_b = reads[:, 3 * pitch + P - 512 : 3 * pitch + P]
         nc.vector.tensor_copy(
             out=hid_b.rearrange("p (h j u) -> p h j u", h=2, u=2),
             in_=turned[:].rearrange("p (h u j) -> p h j u", h=2, u=2),
         )
-        nc.vector.tensor_copy(out=h01[:, O : 2 * O], in_=board[1][:].indirect(l4[:]))
+        nc.vector.tensor_copy(out=h1[1], in_=board[1][:].indirect(l4[:]))
         qb_w = tile("qb_w", J, U32)
         qb_s = tile("qb_s", J, U8)
         nc.vector.quantize_mx(out=qb_w[:].bitcast(E5M2), scales=qb_s[:], in_=hid_b.bitcast(BF16))
@@ -196,30 +192,26 @@ def tile_list_joinedreads_kernel(
 
         hid_h = tile("hid_h", 4 * O, BF16)
         hid_h4 = hid_h[:].rearrange("p (o t) -> p o t", t=4)
-        nc.vector.tensor_copy(out=hid_h4[:, :, 0:2], in_=h01[:].rearrange("p (t o) -> p o t", t=2))
-        h2 = h23[:, 128 : 128 + O]
-        h3 = h23[:, 128 + O : 128 + 2 * O]
-        nc.vector.tensor_copy(out=h2, in_=board[2][:].indirect(l4[:]))
-        nc.vector.tensor_copy(out=h3[:, 0:128], in_=board[3][:].indirect(l4[:, 0:8]))
-        nc.scalar.activation(out=h3[:, 128:256], in_=board[3][:].indirect(l4[:, 8:16]), func=COPY)
+        planes = reads[:].rearrange("p (t s) -> p s t", t=4)
+        nc.vector.tensor_copy(out=h1[2], in_=board[2][:].indirect(l4[:]))
+        nc.vector.tensor_copy(out=h1[3][:, 0:P], in_=board[3][:].indirect(l4[:, 0:8]))
+        nc.scalar.activation(out=h1[3][:, P:O], in_=board[3][:].indirect(l4[:, 8:16]), func=COPY)
+        nc.vector.tensor_copy(out=hid_h4[:, 0:P, :], in_=planes[:, 0:P, :])
+        nc.scalar.copy(out=hid_h4[:, P:O, :], in_=planes[:, P:O, :])
 
         out_v = out.rearrange("(m p) d -> p m d", m=2)
         res_b = tile("res_b", 2 * J, F32)
         nc.scalar.copy(out=res_b[:], in_=out_b[:])
         nc.sync.dma_start(out=out_v[:, :, 0:J], in_=res_b[:].rearrange("p (m d) -> p m d", m=2))
 
-        pairs23 = h23[:, 128 : 128 + 2 * O].rearrange("p (t o) -> p o t", t=2)
         qh_w = tile("qh_w", O, U32)
         qh_s = tile("qh_s", O, U8)
-        for h in range(2):
-            cols = slice(P * h, P * (h + 1))
-            nc.vector.tensor_copy(out=hid_h4[:, cols, 2:4], in_=pairs23[:, cols, :])
         for h in range(2):
             cols = slice(P * h, P * (h + 1))
             nc.vector.quantize_mx(
                 out=qh_w[:, cols].bitcast(E5M2), scales=qh_s[:, cols], in_=hid_h[:, 512 * h : 512 * (h + 1)]
             )
-        out_h = [bank("out_h0"), bank("out_h1")]
+        out_h = [bank("out_h0"), bank("out_h1", tag="a0")]
         res_h = [tile("res_h%d" % h, 2 * P, F32) for h in range(2)]
         for h in range(2):
             cols = slice(P * h, P * (h + 1))

@@ -132,7 +132,10 @@ def tile_list_joinedreads_kernel(
                     stop=True,
                 )
             width = sum(hi - lo for t, lo, hi in group)
-            nc.scalar.copy(out=a_sb[:, first : first + width], in_=a_ps[:, 0:width])
+            if g == 0:
+                nc.scalar.copy(out=a_sb[:, first : first + width], in_=a_ps[:, 0:width])
+            else:
+                nc.vector.tensor_copy(out=a_sb[:, first : first + width], in_=a_ps[:, 0:width])
             for t, lo, hi in group:
                 nc.scalar.activation(
                     out=board[t][:].indirect(l3[:, lo // 16 : hi // 16]),
@@ -147,7 +150,7 @@ def tile_list_joinedreads_kernel(
         nc.vector.tensor_copy(out=xo_gw[:], in_=xo_w[:].indirect(l2[:]))
         spread_rows(nc, late[:, 0 : 2 * R + N].bitcast(I32), late_rows, 1)
 
-        pitch = 640
+        pitch = O
         reads = tile("reads", 4 * pitch, F32, tag="fold_then_h01")
         h1 = [reads[:, pitch * t : pitch * t + O] for t in range(4)]
         nc.vector.tensor_copy(out=h1[0], in_=board[0][:].indirect(l4[:]))
@@ -173,7 +176,8 @@ def tile_list_joinedreads_kernel(
             for u in range(2):
                 k = 2 * h + u
                 nc.tensor.transpose(turned[:, P * k : P * (k + 1)], bt_words[h][:, P * u : P * (u + 1)], ident[:])
-        hid_b = reads[:, 3 * pitch + P - 512 : 3 * pitch + P]
+        hid_b_tile = tile("hid_b", 2 * J, F32)
+        hid_b = hid_b_tile[:]
         nc.vector.tensor_copy(
             out=hid_b.rearrange("p (h j u) -> p h j u", h=2, u=2),
             in_=turned[:].rearrange("p (h u j) -> p h j u", h=2, u=2),
@@ -190,20 +194,22 @@ def tile_list_joinedreads_kernel(
                 rhs=qb_w[:].bitcast(E5M2), rhs_scale=qb_s[:], start=True, stop=True,
             )
 
-        hid_h = tile("hid_h", 4 * O, BF16)
+        hid_h = tile("hid_h", 4 * O, BF16, tag="qb_w")
         hid_h4 = hid_h[:].rearrange("p (o t) -> p o t", t=4)
         planes = reads[:].rearrange("p (t s) -> p s t", t=4)
         nc.vector.tensor_copy(out=h1[2], in_=board[2][:].indirect(l4[:]))
-        nc.vector.tensor_copy(out=h1[3][:, 0:P], in_=board[3][:].indirect(l4[:, 0:8]))
-        nc.scalar.activation(out=h1[3][:, P:O], in_=board[3][:].indirect(l4[:, 8:16]), func=COPY)
-        nc.vector.tensor_copy(out=hid_h4[:, 0:P, :], in_=planes[:, 0:P, :])
-        nc.scalar.copy(out=hid_h4[:, P:O, :], in_=planes[:, P:O, :])
+        for h in range(2):
+            nc.scalar.activation(
+                out=h1[3][:, P * h : P * (h + 1)], in_=board[3][:].indirect(l4[:, 8 * h : 8 * (h + 1)]), func=COPY
+            )
 
         out_v = out.rearrange("(m p) d -> p m d", m=2)
         res_b = tile("res_b", 2 * J, F32)
-        nc.scalar.copy(out=res_b[:], in_=out_b[:])
+        nc.vector.tensor_copy(out=res_b[:], in_=out_b[:])
         nc.sync.dma_start(out=out_v[:, :, 0:J], in_=res_b[:].rearrange("p (m d) -> p m d", m=2))
 
+        for h in range(2):
+            nc.vector.tensor_copy(out=hid_h4[:, P * h : P * (h + 1), :], in_=planes[:, P * h : P * (h + 1), :])
         qh_w = tile("qh_w", O, U32)
         qh_s = tile("qh_s", O, U8)
         for h in range(2):

@@ -23,13 +23,31 @@ def words_of(dram):
     return dram[0].rearrange("p c r -> p (c r)").bitcast(I32)
 
 
-def load_rows(queue, staged, dram):
-    queue.dma_start(out=staged, in_=dram[0].bitcast(I32).rearrange("(q r) n -> r q n", q=4))
+def load_plane(queue, plane, dram):
+    rows = dram[0].bitcast(I32)
+    for q in range(4):
+        queue.dma_start(out=plane[32 * q : 32 * q + 4, :].bitcast(I32), in_=rows[4 * q : 4 * q + 4, :])
 
 
-def spread_rows(nc, plane, staged, first):
-    for q in range(first, 4):
-        nc.vector.tensor_copy(out=plane[32 * q : 32 * q + 4, :], in_=staged[:, q, :])
+def load_folded(queue, folded, dram, first=0):
+    rows = dram[0].bitcast(I32).rearrange("(h b r) n -> b r h n", h=2, b=2)
+    width = rows.shape[3]
+    for b in range(2):
+        halves = folded[32 * b : 32 * b + 4, :].bitcast(I32).rearrange("p (h n) -> p h n", h=2)
+        queue.dma_start(out=halves[:, :, first : first + width], in_=rows[b])
+
+
+def unfold(nc, folded):
+    words = folded[:].bitcast(I32)
+    half = words.shape[1] // 2
+    nc.vector.tensor_copy(out=words[64:128, 0:half], in_=words[0:64, half : 2 * half])
+
+
+def unfold_into(nc, plane, folded):
+    words = folded[:].bitcast(I32)
+    half = words.shape[1] // 2
+    for h in range(2):
+        nc.vector.tensor_copy(out=plane[64 * h : 64 * h + 64, :].bitcast(I32), in_=words[0:64, half * h : half * (h + 1)])
 
 
 def tile_list_joinedreads_kernel(
@@ -58,54 +76,50 @@ def tile_list_joinedreads_kernel(
         xo_w = tile("xo_w", T, U32, tag="fold_then_h01")
         xo_s = tile("xo_s", T, U8)
         w_w = tile("w_w", R, U32)
-        w_s = tile("w_s", R, U8)
+        w_s = tile("w_s", 2 * R, U8)
         w2_w = tile("w2_w", R, U32)
         w0_w = tile("w0_w", R, U32)
+        w2_s = tile("w2_s", R, U8)
+        w0_s = tile("w0_s", R, U8)
         wb_w = tile("wb_w", N, U32)
-
-        def staging(name, width):
-            rows = sb.tile([4, width], I32, name=name)
-            return rows[:].rearrange("p (q n) -> p q n", q=4)
-
-        xt_rows, xo_rows, w_rows = staging("xt_rows", T), staging("xo_rows", T), staging("w_rows", R)
-        late = tile("late", 4 * (2 * R + N), U8)
-        late_rows = late[0:4, :].bitcast(I32).rearrange("p (q n) -> p q n", q=4)
-        w2_s, w0_s, wb_s = late[:, 0:R], late[:, R : 2 * R], late[:, 2 * R : 2 * R + N]
+        wb_s = tile("wb_s", N, U8)
+        xt_f = tile("xt_f", 2 * T, U8)
         board = [tile("board%d" % t, C, F32) for t in range(4)]
         ident = tile("ident", P, F32)
 
+        for folded in (w_s, xt_f):
+            nc.gpsimd.memset(folded[:].bitcast(I32), 0)
+        nc.vector.memset(xo_s[:].bitcast(I32), 0)
+
         nc.sync.dma_start(l1[:], offs)
-        load_rows(nc.sync, xt_rows, xt_scales)
-        load_rows(nc.sync, w_rows, w_scales)
-        nc.sync.dma_start(l2[:], offs2)
         nc.sync.dma_start(out=xt_w[:].bitcast(I32), in_=xt_words[0].bitcast(I32))
         nc.sync.dma_start(out=w_w[:].bitcast(I32), in_=words_of(w_words))
-        load_rows(nc.sync, xo_rows, xo_scales)
+        load_folded(nc.sync, w_s, w_scales)
+        load_folded(nc.sync, xt_f, xt_scales)
         nc.sync.dma_start(out=xo_w[:].bitcast(I32), in_=words_of(xo_words))
         nc.sync.dma_start(l3[:], offs3)
+        nc.sync.dma_start(l2[:], offs2)
+        load_plane(nc.sync, xo_s, xo_scales)
         nc.sync.dma_start(out=w2_w[:].bitcast(I32), in_=words_of(w2_words))
         nc.sync.dma_start(out=w0_w[:].bitcast(I32), in_=words_of(w0_words))
-        load_rows(nc.sync, late_rows[:, :, 0:128], w2_scales)
-        load_rows(nc.sync, late_rows[:, :, 128:256], w0_scales)
-        load_rows(nc.sync, late_rows[:, :, 256:320], wb_scales)
+        load_plane(nc.sync, w2_s, w2_scales)
+        load_plane(nc.sync, w0_s, w0_scales)
         nc.sync.dma_start(l4[:], offs4)
         nc.sync.dma_start(out=wb_w[:].bitcast(I32), in_=words_of(wb_words))
+        load_plane(nc.sync, wb_s, wb_scales)
 
-        for plane in (xt_s, w_s, xo_s):
-            nc.vector.memset(plane[:].bitcast(I32), 0)
-        nc.vector.memset(board[0][:], 0.0)
-        for t in range(1, 4):
-            nc.gpsimd.memset(board[t][:], 0.0)
+        for t in range(3):
+            nc.vector.memset(board[t][:], 0.0)
         make_identity(nc, ident[:])
+        nc.gpsimd.memset(board[3][:], 0.0)
 
         xt_gw = tile("xt_gw", J, U16)
         xt_gs = tile("xt_gs", J, U8)
-        spread_rows(nc, xt_s[:].bitcast(I32), xt_rows, 0)
-        spread_rows(nc, w_s[:].bitcast(I32), w_rows, 0)
+        nc.vector.tensor_copy(out=xt_gw[:], in_=xt_w[:].indirect(l1[:]))
+        unfold(nc, w_s)
+        unfold_into(nc, xt_s, xt_f)
         for h in range(2):
-            entries = l1[:, 8 * h : 8 * (h + 1)]
-            nc.vector.tensor_copy(out=xt_gs[:, P * h : P * (h + 1)], in_=xt_s[:].indirect(entries))
-            nc.vector.tensor_copy(out=xt_gw[:, P * h : P * (h + 1)], in_=xt_w[:].indirect(entries))
+            nc.vector.tensor_copy(out=xt_gs[:, P * h : P * (h + 1)], in_=xt_s[:].indirect(l1[:, 8 * h : 8 * (h + 1)]))
 
         w_pw = [tile("w_pw%d" % t, P, U32) for t in range(4)]
         w_ps = [tile("w_ps%d" % t, P, U8) for t in range(4)]
@@ -132,7 +146,7 @@ def tile_list_joinedreads_kernel(
                     stop=True,
                 )
             width = sum(hi - lo for t, lo, hi in group)
-            if g == 0:
+            if g < 2:
                 nc.scalar.copy(out=a_sb[:, first : first + width], in_=a_ps[:, 0:width])
             else:
                 nc.vector.tensor_copy(out=a_sb[:, first : first + width], in_=a_ps[:, 0:width])
@@ -145,12 +159,10 @@ def tile_list_joinedreads_kernel(
 
         xo_gw = tile("xo_gw", J, U32)
         xo_gs = tile("xo_gs", J, U8)
-        spread_rows(nc, xo_s[:].bitcast(I32), xo_rows, 0)
         nc.vector.tensor_copy(out=xo_gs[:], in_=xo_s[:].indirect(l2[:]))
         nc.vector.tensor_copy(out=xo_gw[:], in_=xo_w[:].indirect(l2[:]))
-        spread_rows(nc, late[:, 0 : 2 * R + N].bitcast(I32), late_rows, 1)
 
-        pitch = O
+        pitch = 640
         reads = tile("reads", 4 * pitch, F32, tag="fold_then_h01")
         h1 = [reads[:, pitch * t : pitch * t + O] for t in range(4)]
         nc.vector.tensor_copy(out=h1[0], in_=board[0][:].indirect(l4[:]))
@@ -162,11 +174,11 @@ def tile_list_joinedreads_kernel(
             bt = bank("bt%d" % h)
             nc.tensor.matmul_mx(
                 out=bt[:], lhsT=xt_gw[:, cols].bitcast(E2M1), lhsT_scale=xt_gs[:, cols],
-                rhs=w2_w[:].bitcast(E4M3), rhs_scale=w2_s, start=True, stop=False,
+                rhs=w2_w[:].bitcast(E4M3), rhs_scale=w2_s[:], start=True, stop=False,
             )
             nc.tensor.matmul_mx(
                 out=bt[:], lhsT=xo_gw[:, cols].bitcast(E5M2), lhsT_scale=xo_gs[:, cols],
-                rhs=w0_w[:].bitcast(E4M3), rhs_scale=w0_s, start=False, stop=True,
+                rhs=w0_w[:].bitcast(E4M3), rhs_scale=w0_s[:], start=False, stop=True,
             )
             nc.vector.tensor_copy(
                 out=bt_words[h].bitcast(BF16).rearrange("j (u p e) -> j u p e", u=2, e=2),
@@ -176,8 +188,7 @@ def tile_list_joinedreads_kernel(
             for u in range(2):
                 k = 2 * h + u
                 nc.tensor.transpose(turned[:, P * k : P * (k + 1)], bt_words[h][:, P * u : P * (u + 1)], ident[:])
-        hid_b_tile = tile("hid_b", 2 * J, F32)
-        hid_b = hid_b_tile[:]
+        hid_b = reads[:, 3 * pitch + P - 512 : 3 * pitch + P]
         nc.vector.tensor_copy(
             out=hid_b.rearrange("p (h j u) -> p h j u", h=2, u=2),
             in_=turned[:].rearrange("p (h u j) -> p h j u", h=2, u=2),
@@ -194,22 +205,20 @@ def tile_list_joinedreads_kernel(
                 rhs=qb_w[:].bitcast(E5M2), rhs_scale=qb_s[:], start=True, stop=True,
             )
 
-        hid_h = tile("hid_h", 4 * O, BF16, tag="qb_w")
+        hid_h = tile("hid_h", 4 * O, BF16)
         hid_h4 = hid_h[:].rearrange("p (o t) -> p o t", t=4)
         planes = reads[:].rearrange("p (t s) -> p s t", t=4)
         nc.vector.tensor_copy(out=h1[2], in_=board[2][:].indirect(l4[:]))
-        for h in range(2):
-            nc.scalar.activation(
-                out=h1[3][:, P * h : P * (h + 1)], in_=board[3][:].indirect(l4[:, 8 * h : 8 * (h + 1)]), func=COPY
-            )
+        nc.vector.tensor_copy(out=h1[3][:, 0:P], in_=board[3][:].indirect(l4[:, 0:8]))
+        nc.scalar.activation(out=h1[3][:, P:O], in_=board[3][:].indirect(l4[:, 8:16]), func=COPY)
+        nc.vector.tensor_copy(out=hid_h4[:, 0:P, :], in_=planes[:, 0:P, :])
+        nc.scalar.copy(out=hid_h4[:, P:O, :], in_=planes[:, P:O, :])
 
         out_v = out.rearrange("(m p) d -> p m d", m=2)
         res_b = tile("res_b", 2 * J, F32)
-        nc.vector.tensor_copy(out=res_b[:], in_=out_b[:])
+        nc.scalar.copy(out=res_b[:], in_=out_b[:])
         nc.sync.dma_start(out=out_v[:, :, 0:J], in_=res_b[:].rearrange("p (m d) -> p m d", m=2))
 
-        for h in range(2):
-            nc.vector.tensor_copy(out=hid_h4[:, P * h : P * (h + 1), :], in_=planes[:, P * h : P * (h + 1), :])
         qh_w = tile("qh_w", O, U32)
         qh_s = tile("qh_s", O, U8)
         for h in range(2):

from contextlib import ExitStack

import concourse.mybir as mybir
from concourse.masks import make_identity

F32 = mybir.dt.float32
BF16 = mybir.dt.bfloat16
I32 = mybir.dt.int32
U32 = mybir.dt.uint32
U16 = mybir.dt.uint16
U8 = mybir.dt.uint8
E4M3 = mybir.dt.float8_e4m3fn_x4
E5M2 = mybir.dt.float8_e5m2_x4
E2M1 = mybir.dt.float4_e2m1fn_x4
COPY = mybir.ActivationFunctionType.Copy

P = 128
T, J, R, C, O, N = 1024, 256, 512, 512, 256, 256
FLOPS = 536870912


def words_of(dram):
    return dram[0].rearrange("p c r -> p (c r)").bitcast(I32)


def load_plane(queue, plane, dram):
    rows = dram[0].bitcast(I32)
    for q in range(4):
        queue.dma_start(out=plane[32 * q : 32 * q + 4, :].bitcast(I32), in_=rows[4 * q : 4 * q + 4, :])


def load_folded(queue, folded, dram, first=0):
    rows = dram[0].bitcast(I32).rearrange("(h b r) n -> b r h n", h=2, b=2)
    width = rows.shape[3]
    for b in range(2):
        halves = folded[32 * b : 32 * b + 4, :].bitcast(I32).rearrange("p (h n) -> p h n", h=2)
        queue.dma_start(out=halves[:, :, first : first + width], in_=rows[b])


def unfold(nc, folded):
    words = folded[:].bitcast(I32)
    half = words.shape[1] // 2
    nc.vector.tensor_copy(out=words[64:128, 0:half], in_=words[0:64, half : 2 * half])


def unfold_into(nc, plane, folded):
    words = folded[:].bitcast(I32)
    half = words.shape[1] // 2
    for h in range(2):
        nc.vector.tensor_copy(out=plane[64 * h : 64 * h + 64, :].bitcast(I32), in_=words[0:64, half * h : half * (h + 1)])


def tile_list_joinedreads_kernel(
    tc, xt_words, xt_scales, xo_words, xo_scales, w_words, w_scales, w2_words, w2_scales,
    w0_words, w0_scales, wb_words, wb_scales, offs, offs2, offs3, offs4, out,
):
    nc = tc.nc
    with ExitStack() as ctx:
        lists = ctx.enter_context(tc.tile_pool(name="lists", bufs=1))
        sb = ctx.enter_context(tc.tile_pool(name="sb", bufs=1))
        ps = ctx.enter_context(tc.psum_pool(name="ps", bufs=1))

        def tile(name, width, dtype, tag=None):
            return sb.tile([P, width], dtype, name=name, tag=tag or name, align_bytes=64)

        def bank(name, tag=None):
            return ps.tile([P, 512], F32, name=name, tag=tag or name)

        l1 = lists.tile([P, 16], U16, name="l1")
        l2 = lists.tile([P, 16], U16, name="l2")
        l3 = lists.tile([P, 16], U16, name="l3")
        l4 = lists.tile([P, 16], U16, name="l4")

        xt_w = tile("xt_w", T, U16)
        xt_s = tile("xt_s", T, U8)
        xo_w = tile("xo_w", T, U32, tag="fold_then_h01")
        xo_s = tile("xo_s", T, U8)
        w_w = tile("w_w", R, U32)
        w_s = tile("w_s", 2 * R, U8)
        w2_w = tile("w2_w", R, U32)
        w0_w = tile("w0_w", R, U32)
        w2_s = tile("w2_s", R, U8)
        w0_s = tile("w0_s", R, U8)
        wb_w = tile("wb_w", N, U32)
        wb_s = tile("wb_s", N, U8)
        xt_f = tile("xt_f", 2 * T, U8)
        board = [tile("board%d" % t, C, F32) for t in range(4)]
        ident = tile("ident", P, F32)

        for folded in (w_s, xt_f):
            nc.gpsimd.memset(folded[:].bitcast(I32), 0)
        nc.vector.memset(xo_s[:].bitcast(I32), 0)

        nc.sync.dma_start(l1[:], offs)
        nc.sync.dma_start(out=xt_w[:].bitcast(I32), in_=xt_words[0].bitcast(I32))
        nc.sync.dma_start(out=w_w[:].bitcast(I32), in_=words_of(w_words))
        load_folded(nc.sync, w_s, w_scales)
        load_folded(nc.sync, xt_f, xt_scales)
        nc.sync.dma_start(out=xo_w[:].bitcast(I32), in_=words_of(xo_words))
        nc.sync.dma_start(l3[:], offs3)
        nc.sync.dma_start(l2[:], offs2)
        load_plane(nc.sync, xo_s, xo_scales)
        nc.sync.dma_start(out=w2_w[:].bitcast(I32), in_=words_of(w2_words))
        nc.sync.dma_start(out=w0_w[:].bitcast(I32), in_=words_of(w0_words))
        load_plane(nc.sync, w2_s, w2_scales)
        load_plane(nc.sync, w0_s, w0_scales)
        nc.sync.dma_start(l4[:], offs4)
        nc.sync.dma_start(out=wb_w[:].bitcast(I32), in_=words_of(wb_words))
        load_plane(nc.sync, wb_s, wb_scales)

        for t in range(3):
            nc.vector.memset(board[t][:], 0.0)
        make_identity(nc, ident[:])
        nc.gpsimd.memset(board[3][:], 0.0)

        xt_gw = tile("xt_gw", J, U16)
        xt_gs = tile("xt_gs", J, U8)
        nc.vector.tensor_copy(out=xt_gw[:], in_=xt_w[:].indirect(l1[:]))
        unfold(nc, w_s)
        unfold_into(nc, xt_s, xt_f)
        for h in range(2):
            nc.vector.tensor_copy(out=xt_gs[:, P * h : P * (h + 1)], in_=xt_s[:].indirect(l1[:, 8 * h : 8 * (h + 1)]))

        w_pw = [tile("w_pw%d" % t, P, U32) for t in range(4)]
        w_ps = [tile("w_ps%d" % t, P, U8) for t in range(4)]
        w_w4 = w_w[:].rearrange("p (m t) -> p t m", t=4)
        w_s4 = w_s[:, 0:R].rearrange("p (m t) -> p t m", t=4)
        for t in range(4):
            nc.gpsimd.tensor_copy(out=w_ps[t][:], in_=w_s4[:, t, :])
            nc.scalar.copy(out=w_pw[t][:], in_=w_w4[:, t, :])

        a_sb = tile("a_sb", 4 * J, F32)
        pieces = [(0, 0, P), (0, P, J), (1, 0, J), (2, 0, J), (3, 0, J)]
        groups = [pieces[0:1], pieces[1:3], pieces[3:5]]
        for g, group in enumerate(groups):
            a_ps = bank("a%d" % g)
            first = J * group[0][0] + group[0][1]
            for t, lo, hi in group:
                nc.tensor.matmul_mx(
                    out=a_ps[:, J * t + lo - first : J * t + hi - first],
                    lhsT=w_pw[t][:].bitcast(E5M2),
                    lhsT_scale=w_ps[t][:],
                    rhs=xt_gw[:, lo:hi].bitcast(E2M1),
                    rhs_scale=xt_gs[:, lo:hi],
                    start=True,
                    stop=True,
                )
            width = sum(hi - lo for t, lo, hi in group)
            if g < 2:
                nc.scalar.copy(out=a_sb[:, first : first + width], in_=a_ps[:, 0:width])
            else:
                nc.vector.tensor_copy(out=a_sb[:, first : first + width], in_=a_ps[:, 0:width])
            for t, lo, hi in group:
                nc.scalar.activation(
                    out=board[t][:].indirect(l3[:, lo // 16 : hi // 16]),
                    in_=a_sb[:, J * t + lo : J * t + hi],
                    func=COPY,
                )

        xo_gw = tile("xo_gw", J, U32)
        xo_gs = tile("xo_gs", J, U8)
        nc.vector.tensor_copy(out=xo_gs[:], in_=xo_s[:].indirect(l2[:]))
        nc.vector.tensor_copy(out=xo_gw[:], in_=xo_w[:].indirect(l2[:]))

        pitch = 640
        reads = tile("reads", 4 * pitch, F32, tag="fold_then_h01")
        h1 = [reads[:, pitch * t : pitch * t + O] for t in range(4)]
        nc.vector.tensor_copy(out=h1[0], in_=board[0][:].indirect(l4[:]))

        bt_words = [h1[1], h1[2]]
        turned = bank("turned")
        for h in range(2):
            cols = slice(P * h, P * (h + 1))
            bt = bank("bt%d" % h)
            nc.tensor.matmul_mx(
                out=bt[:], lhsT=xt_gw[:, cols].bitcast(E2M1), lhsT_scale=xt_gs[:, cols],
                rhs=w2_w[:].bitcast(E4M3), rhs_scale=w2_s[:], start=True, stop=False,
            )
            nc.tensor.matmul_mx(
                out=bt[:], lhsT=xo_gw[:, cols].bitcast(E5M2), lhsT_scale=xo_gs[:, cols],
                rhs=w0_w[:].bitcast(E4M3), rhs_scale=w0_s[:], start=False, stop=True,
            )
            nc.vector.tensor_copy(
                out=bt_words[h].bitcast(BF16).rearrange("j (u p e) -> j u p e", u=2, e=2),
                in_=bt[:].rearrange("j (p u e) -> j u p e", u=2, e=2),
            )
        for h in range(2):
            for u in range(2):
                k = 2 * h + u
                nc.tensor.transpose(turned[:, P * k : P * (k + 1)], bt_words[h][:, P * u : P * (u + 1)], ident[:])
        hid_b = reads[:, 3 * pitch + P - 512 : 3 * pitch + P]
        nc.vector.tensor_copy(
            out=hid_b.rearrange("p (h j u) -> p h j u", h=2, u=2),
            in_=turned[:].rearrange("p (h u j) -> p h j u", h=2, u=2),
        )
        nc.vector.tensor_copy(out=h1[1], in_=board[1][:].indirect(l4[:]))
        qb_w = tile("qb_w", J, U32)
        qb_s = tile("qb_s", J, U8)
        nc.vector.quantize_mx(out=qb_w[:].bitcast(E5M2), scales=qb_s[:], in_=hid_b.bitcast(BF16))
        out_b = bank("out_b")
        for m in range(2):
            nc.tensor.matmul_mx(
                out=out_b[:, J * m : J * (m + 1)],
                lhsT=wb_w[:, P * m : P * (m + 1)].bitcast(E4M3), lhsT_scale=wb_s[:, P * m : P * (m + 1)],
                rhs=qb_w[:].bitcast(E5M2), rhs_scale=qb_s[:], start=True, stop=True,
            )

        hid_h = tile("hid_h", 4 * O, BF16)
        hid_h4 = hid_h[:].rearrange("p (o t) -> p o t", t=4)
        planes = reads[:].rearrange("p (t s) -> p s t", t=4)
        nc.vector.tensor_copy(out=h1[2], in_=board[2][:].indirect(l4[:]))
        nc.vector.tensor_copy(out=h1[3][:, 0:P], in_=board[3][:].indirect(l4[:, 0:8]))
        nc.scalar.activation(out=h1[3][:, P:O], in_=board[3][:].indirect(l4[:, 8:16]), func=COPY)
        nc.vector.tensor_copy(out=hid_h4[:, 0:P, :], in_=planes[:, 0:P, :])
        nc.scalar.copy(out=hid_h4[:, P:O, :], in_=planes[:, P:O, :])

        out_v = out.rearrange("(m p) d -> p m d", m=2)
        res_b = tile("res_b", 2 * J, F32)
        nc.scalar.copy(out=res_b[:], in_=out_b[:])
        nc.sync.dma_start(out=out_v[:, :, 0:J], in_=res_b[:].rearrange("p (m d) -> p m d", m=2))

        qh_w = tile("qh_w", O, U32)
        qh_s = tile("qh_s", O, U8)
        for h in range(2):
            cols = slice(P * h, P * (h + 1))
            nc.vector.quantize_mx(
                out=qh_w[:, cols].bitcast(E5M2), scales=qh_s[:, cols], in_=hid_h[:, 512 * h : 512 * (h + 1)]
            )
        out_h = [bank("out_h0"), bank("out_h1", tag="a0")]
        res_h = [tile("res_h%d" % h, 2 * P, F32) for h in range(2)]
        for h in range(2):
            cols = slice(P * h, P * (h + 1))
            for m in range(2):
                nc.tensor.matmul_mx(
                    out=out_h[h][:, P * m : P * (m + 1)],
                    lhsT=wb_w[:, P * m : P * (m + 1)].bitcast(E4M3), lhsT_scale=wb_s[:, P * m : P * (m + 1)],
                    rhs=qh_w[:, cols].bitcast(E5M2), rhs_scale=qh_s[:, cols], start=True, stop=True,
                )
        nc.scalar.copy(out=res_h[0][:], in_=out_h[0][:, 0 : 2 * P])
        nc.scalar.dma_start(out=out_v[:, :, J : J + P], in_=res_h[0][:].rearrange("p (m d) -> p m d", m=2))
        nc.vector.tensor_copy(out=res_h[1][:], in_=out_h[1][:, 0 : 2 * P])
        nc.sync.dma_start(out=out_v[:, :, J + P : J + 2 * P], in_=res_h[1][:].rearrange("p (m d) -> p m d", m=2))
